import numpy as np
import ml_dtypes


def mxq(x, axis, fmt="e4m3"):
    dtype, down = {"e4m3": (ml_dtypes.float8_e4m3fn, 7), "e5m2": (ml_dtypes.float8_e5m2, 14)}[fmt]
    v = np.moveaxis(np.asarray(x, np.float32).astype(ml_dtypes.bfloat16).astype(np.float64), axis, -1)
    blocks = v.reshape(v.shape[:-1] + (-1, 32))
    amax = np.abs(blocks).max(-1, keepdims=True)
    byte = np.maximum(np.where(amax > 0, np.frexp(amax)[1] - 1 + 127, 0) - down, 1)
    scale = np.exp2(byte - 127.0)
    codes = (blocks / scale).astype(np.float32).astype(dtype).astype(np.float64)
    return np.moveaxis((codes * scale).reshape(v.shape), -1, axis)


WIDE = False


def mx_kscale(k, group=512):
    if not WIDE:
        return np.ones(k)
    levels = np.array([18, -18])
    if group != 512:
        return np.exp2(np.random.permutation(np.resize(levels, k // group))).repeat(group)
    if k % 512:
        return np.exp2(np.random.permutation(np.resize(levels, k // 32))).repeat(32)
    a = np.empty((k // 512, 16))
    for p in range(k // 512):
        a[p, :8] = np.random.permutation(np.resize(levels, 8))
        for g in range(8):
            far = levels[np.abs(levels - a[p, g]) >= 10]
            a[p, g + 8] = far[np.random.randint(len(far))]
    return np.exp2(a.ravel()).repeat(32)


def f64(x):
    return np.asarray(x).astype(np.float64)


E2M1 = np.array([0.0, 0.5, 1.0, 1.5, 2.0, 3.0, 4.0, 6.0, -0.0, -0.5, -1.0, -1.5, -2.0, -3.0, -4.0, -6.0])


def pack_group(w):
    k, n = w.shape
    w = f64(np.asarray(w, np.float32).astype(ml_dtypes.bfloat16)).reshape(k // 32, 32, n)
    amax = np.abs(w).max(1)
    mant, ex = np.frexp(amax / 6.0)
    byte = np.clip(np.where(amax > 0, np.where(mant > 0.5, ex, ex - 1) + 127, 1), 1, 254)
    scaled = (w * np.exp2(127.0 - byte)[:, None, :]).reshape(k, n).astype(np.float32)
    c = np.ascontiguousarray(scaled.reshape(k // 4, 4, n).transpose(0, 2, 1)).astype(ml_dtypes.float4_e2m1fn).view(np.uint8) & 0xF
    return np.ascontiguousarray((c[..., 0::2] | (c[..., 1::2] << 4)).reshape(k // 4, 2 * n)), byte.astype(np.uint8)


def unpack_group(words, scales):
    p, n = words.shape[0], scales.shape[1]
    words = np.ascontiguousarray(words).reshape(p, n, 2)
    nib = np.empty((p, n, 4), np.uint8)
    nib[..., 0::2] = words & 0xF
    nib[..., 1::2] = words >> 4
    return E2M1[nib].transpose(0, 2, 1).reshape(4 * p, n) * np.repeat(np.exp2(scales.astype(np.float64) - 127.0), 32, axis=0)


def gelu(v):
    return 0.5 * v * (1.0 + np.tanh(0.7978845608028654 * (v + 0.044715 * v ** 3)))


G, D, M, N = 8, 128, 128, 512


def setup_inputs():
    n = np.random.standard_normal
    s = mx_kscale(D, 0)[:, None]
    w_ = [pack_group(w) for w in n((G, D, M)) / np.sqrt(D) / s]
    return {
        "x": (n((G, D, N)) * s).astype(np.float32),
        "w_words": np.stack([w[0] for w in w_]),
        "w_scales": np.stack([w[1] for w in w_]),
        "b": (0.5 * n((G, M, 1))).astype(np.float32),
    }


def reference(x, w_words, w_scales, b):
    xq = mxq(f64(x), 1, "e4m3")
    y = np.stack([unpack_group(w_words[g], w_scales[g]) for g in range(G)]).transpose(0, 2, 1) @ xq
    y = y + f64(b)
    y = gelu(y)
    return y

@@ -1,0 +1,114 @@
+from contextlib import ExitStack
+
+import concourse.mybir as mybir
+
+G, D, M, N = 8, 128, 128, 512
+FLOPS = 2 * G * D * M * N
+
+F32 = mybir.dt.float32
+BF16 = mybir.dt.bfloat16
+I32 = mybir.dt.int32
+U32 = mybir.dt.uint32
+U8 = mybir.dt.uint8
+FP8X4 = mybir.dt.float8_e4m3fn_x4
+FP4X4 = mybir.dt.float4_e2m1fn_x4
+GELU = mybir.ActivationFunctionType.Gelu_apprx_tanh
+
+P = 128
+PACK = 4
+ROWS = D // PACK
+TILES = P // ROWS
+SETS = G // TILES
+STAGES = [(0, 0, 256), (0, 256, 256), (1, 0, 256), (1, 256, 256)]
+QCOLS = 128
+STORES = [[2, 2], [2, 2], [2, 2], [2, 1, 1]]
+
+
+def tile_rows_glin_gelu_bias_kernel(tc, x, w_words, w_scales, b, out):
+    nc = tc.nc
+    pad = N - STAGES[0][2]
+    with ExitStack() as ctx:
+        keep = ctx.enter_context(tc.tile_pool(name="keep", bufs=1))
+        psum = ctx.enter_context(tc.psum_pool(name="psum", bufs=1))
+        ctx.enter_context(tc.manual_schedule())
+
+        w_codes = keep.tile([P, SETS, 2 * M], U8, align_bytes=64)
+        w_plane = keep.tile([P, SETS, M], U8, align_bytes=64)
+        b_rows = keep.tile([P, G * 32], F32, align_bytes=64)
+        b_cols = keep.tile([P, G * 32], F32, align_bytes=64)
+        x_codes = keep.tile([P, pad + SETS * N], U32, align_bytes=64)
+        x_plane = keep.tile([P, pad + SETS * N], U8, align_bytes=64)
+        warm_in = keep.tile([P, 1], F32)
+        warm_out = keep.tile([P, 1], F32)
+        raw = [keep.tile([P, PACK, w], F32, name="raw%d" % i) for i, (s, c0, w) in enumerate(STAGES)]
+        packed = [keep.tile([P, w, PACK], BF16, align_bytes=64, name="packed%d" % i) for i, (s, c0, w) in enumerate(STAGES)]
+        res = [keep.tile([P, TILES, w], F32, name="res%d" % i) for i, (s, c0, w) in enumerate(STAGES)]
+        banks = [[psum.tile([M, N], F32, name="bank%d_%d" % (c, k)) for k in range(2)] for c in range(TILES)]
+
+        nc.vector.memset(b_rows[:], 0.0)
+        nc.vector.memset(w_plane[:].rearrange("p s m -> p (s m)").bitcast(I32), 0)
+        nc.gpsimd.memset(warm_in[:], 0.0)
+        nc.vector.memset(x_codes[:, 0:pad], 0)
+        nc.vector.memset(x_plane[:, 0:pad].bitcast(I32), 0)
+
+        nc.scalar.dma_start(out=w_codes[:].bitcast(I32), in_=w_words.rearrange("(s c) p b -> (c p) s b", c=TILES).bitcast(I32))
+
+        def load(i):
+            s, c0, w = STAGES[i]
+            nc.sync.dma_start(
+                out=raw[i][:],
+                in_=x[s * TILES : (s + 1) * TILES].rearrange("c (p j) n -> (c p) j n", j=PACK)[:, :, c0 : c0 + w],
+            )
+
+        load(0)
+        nc.scalar.dma_start(
+            out=b_rows[0:P:32, :].rearrange("q (g i) -> q g i", i=32),
+            in_=b.rearrange("g (q i) o -> q g (i o)", i=32),
+        )
+        scale_rows = w_scales.rearrange("(s c) f m -> c f s m", c=TILES)
+        for c in range(TILES):
+            nc.scalar.dma_start(out=w_plane[ROWS * c : ROWS * c + 4].bitcast(I32), in_=scale_rows[c].bitcast(I32))
+        for i in range(1, len(STAGES)):
+            load(i)
+        nc.scalar.activation(out=warm_out[:], in_=warm_in[:], func=GELU)
+        nc.vector.transpose(out=b_cols[:], in_=b_rows[:])
+
+        for i, (s, c0, w) in enumerate(STAGES):
+            parts = range(0, w, QCOLS)
+            for q in parts:
+                nc.vector.tensor_copy(
+                    out=packed[i][:, q : q + QCOLS, :].rearrange("p (c i) t -> p c t i", i=4),
+                    in_=raw[i][:, :, q : q + QCOLS].rearrange("p t (c i) -> p c t i", i=4),
+                )
+            start = pad + s * N + c0
+            for q in parts:
+                nc.vector.quantize_mx(
+                    out=x_codes[:, start + q : start + q + QCOLS].bitcast(FP8X4),
+                    scales=x_plane[:, start + q : start + q + QCOLS],
+                    in_=packed[i][:, q : q + QCOLS, :].rearrange("p n t -> p (n t)"),
+                )
+            window = slice(start + w - N, start + w)
+            for c in range(TILES):
+                rows = slice(ROWS * c, ROWS * (c + 1))
+                nc.tensor.matmul_mx(
+                    out=banks[c][i % 2][:],
+                    lhsT=w_codes[rows, s, :].bitcast(FP4X4),
+                    lhsT_scale=w_plane[rows, s, :],
+                    rhs=x_codes[rows, window].bitcast(FP8X4),
+                    rhs_scale=x_plane[rows, window],
+                    start=True,
+                    stop=True,
+                )
+            first = 0
+            for count in STORES[i]:
+                for c in range(first, first + count):
+                    g = s * TILES + c
+                    nc.scalar.activation(
+                        out=res[i][:, c, :], in_=banks[c][i % 2][:, N - w : N], func=GELU, bias=b_cols[:, 32 * g : 32 * g + 1]
+                    )
+                g0 = s * TILES + first
+                nc.sync.dma_start(
+                    out=out[g0 : g0 + count, :, c0 : c0 + w].rearrange("g m n -> m g n"),
+                    in_=res[i][:, first : first + count, :],
+                )
+                first += count

@@ -19,9 +19,10 @@ PACK = 4
 ROWS = D // PACK
 TILES = P // ROWS
 SETS = G // TILES
-STAGES = [(0, 0, 256), (0, 256, 256), (1, 0, 256), (1, 256, 256)]
+STAGES = [(0, 0, 512), (1, 0, 512)]
 QCOLS = 128
-STORES = [[2, 2], [2, 2], [2, 2], [2, 1, 1]]
+LOADS = [(0, 0, 256), (0, 256, 256), (1, 0, 256), (1, 256, 256)]
+STORES = [[(c, 1, 0, 512) for c in range(4)], [(0, 1, 0, 512), (1, 1, 0, 512), (2, 1, 0, 512), (3, 1, 0, 256), (3, 1, 256, 512)]]
 
 
 def tile_rows_glin_gelu_bias_kernel(tc, x, w_words, w_scales, b, out):
@@ -40,54 +41,61 @@ def tile_rows_glin_gelu_bias_kernel(tc, x, w_words, w_scales, b, out):
         x_plane = keep.tile([P, pad + SETS * N], U8, align_bytes=64)
         warm_in = keep.tile([P, 1], F32)
         warm_out = keep.tile([P, 1], F32)
-        raw = [keep.tile([P, PACK, w], F32, name="raw%d" % i) for i, (s, c0, w) in enumerate(STAGES)]
-        packed = [keep.tile([P, w, PACK], BF16, align_bytes=64, name="packed%d" % i) for i, (s, c0, w) in enumerate(STAGES)]
+        raw = [keep.tile([P, PACK, w], F32, name="raw%d" % i) for i, (s, c0, w) in enumerate(LOADS)]
+        packed = [keep.tile([P, w, PACK], BF16, align_bytes=64, name="packed%d" % i) for i, (s, c0, w) in enumerate(LOADS)]
         res = [keep.tile([P, TILES, w], F32, name="res%d" % i) for i, (s, c0, w) in enumerate(STAGES)]
         banks = [[psum.tile([M, N], F32, name="bank%d_%d" % (c, k)) for k in range(2)] for c in range(TILES)]
 
-        nc.vector.memset(b_rows[:], 0.0)
         nc.vector.memset(w_plane[:].rearrange("p s m -> p (s m)").bitcast(I32), 0)
-        nc.gpsimd.memset(warm_in[:], 0.0)
-        nc.vector.memset(x_codes[:, 0:pad], 0)
-        nc.vector.memset(x_plane[:, 0:pad].bitcast(I32), 0)
-
-        nc.scalar.dma_start(out=w_codes[:].bitcast(I32), in_=w_words.rearrange("(s c) p b -> (c p) s b", c=TILES).bitcast(I32))
+        nc.vector.memset(warm_in[:], 0.0)
+        nc.gpsimd.memset(b_rows[:], 0.0)
+        nc.gpsimd.dma_start(
+            out=b_rows[0:P:32, :].rearrange("q (g i) -> q g i", i=32),
+            in_=b.rearrange("g (q i) o -> q g (i o)", i=32),
+        )
+        nc.scalar.activation(out=warm_out[:], in_=warm_in[:], func=GELU)
 
         def load(i):
-            s, c0, w = STAGES[i]
+            s, c0, w = LOADS[i]
             nc.sync.dma_start(
                 out=raw[i][:],
                 in_=x[s * TILES : (s + 1) * TILES].rearrange("c (p j) n -> (c p) j n", j=PACK)[:, :, c0 : c0 + w],
             )
 
-        load(0)
-        nc.scalar.dma_start(
-            out=b_rows[0:P:32, :].rearrange("q (g i) -> q g i", i=32),
-            in_=b.rearrange("g (q i) o -> q g (i o)", i=32),
-        )
+        for i in range(2):
+            load(i)
+        nc.sync.dma_start(out=w_codes[:].bitcast(I32), in_=w_words.rearrange("(s c) p b -> (c p) s b", c=TILES).bitcast(I32))
         scale_rows = w_scales.rearrange("(s c) f m -> c f s m", c=TILES)
         for c in range(TILES):
-            nc.scalar.dma_start(out=w_plane[ROWS * c : ROWS * c + 4].bitcast(I32), in_=scale_rows[c].bitcast(I32))
-        for i in range(1, len(STAGES)):
+            nc.sync.dma_start(out=w_plane[ROWS * c : ROWS * c + 4].bitcast(I32), in_=scale_rows[c].bitcast(I32))
+        for i in range(2, len(LOADS)):
             load(i)
-        nc.scalar.activation(out=warm_out[:], in_=warm_in[:], func=GELU)
-        nc.vector.transpose(out=b_cols[:], in_=b_rows[:])
 
-        for i, (s, c0, w) in enumerate(STAGES):
+        def quantise(k):
+            s, c0, w = LOADS[k]
             parts = range(0, w, QCOLS)
             for q in parts:
                 nc.vector.tensor_copy(
-                    out=packed[i][:, q : q + QCOLS, :].rearrange("p (c i) t -> p c t i", i=4),
-                    in_=raw[i][:, :, q : q + QCOLS].rearrange("p t (c i) -> p c t i", i=4),
+                    out=packed[k][:, q : q + QCOLS, :].rearrange("p (c i) t -> p c t i", i=4),
+                    in_=raw[k][:, :, q : q + QCOLS].rearrange("p t (c i) -> p c t i", i=4),
                 )
             start = pad + s * N + c0
             for q in parts:
                 nc.vector.quantize_mx(
                     out=x_codes[:, start + q : start + q + QCOLS].bitcast(FP8X4),
                     scales=x_plane[:, start + q : start + q + QCOLS],
-                    in_=packed[i][:, q : q + QCOLS, :].rearrange("p n t -> p (n t)"),
+                    in_=packed[k][:, q : q + QCOLS, :].rearrange("p n t -> p (n t)"),
                 )
-            window = slice(start + w - N, start + w)
+
+        done = 0
+        for i, (s, c0, w) in enumerate(STAGES):
+            while done < len(LOADS) and LOADS[done][0] * N + LOADS[done][1] < s * N + c0 + w:
+                quantise(done)
+                done += 1
+            if i == 0:
+                nc.vector.transpose(out=b_cols[:], in_=b_rows[:])
+            end = pad + s * N + c0 + w
+            window = slice(end - N, end)
             for c in range(TILES):
                 rows = slice(ROWS * c, ROWS * (c + 1))
                 nc.tensor.matmul_mx(
@@ -99,16 +107,17 @@ def tile_rows_glin_gelu_bias_kernel(tc, x, w_words, w_scales, b, out):
                     start=True,
                     stop=True,
                 )
-            first = 0
-            for count in STORES[i]:
+            for first, count, lo, hi in STORES[i]:
                 for c in range(first, first + count):
                     g = s * TILES + c
                     nc.scalar.activation(
-                        out=res[i][:, c, :], in_=banks[c][i % 2][:, N - w : N], func=GELU, bias=b_cols[:, 32 * g : 32 * g + 1]
+                        out=res[i][:, c, lo:hi],
+                        in_=banks[c][i % 2][:, N - w + lo : N - w + hi],
+                        func=GELU,
+                        bias=b_cols[:, 32 * g : 32 * g + 1],
                     )
                 g0 = s * TILES + first
                 nc.sync.dma_start(
-                    out=out[g0 : g0 + count, :, c0 : c0 + w].rearrange("g m n -> m g n"),
-                    in_=res[i][:, first : first + count, :],
+                    out=out[g0 : g0 + count, :, c0 + lo : c0 + hi].rearrange("g m n -> m g n"),
+                    in_=res[i][:, first : first + count, lo:hi],
                 )
-                first += count

@@ -19,10 +19,10 @@ PACK = 4
 ROWS = D // PACK
 TILES = P // ROWS
 SETS = G // TILES
-STAGES = [(0, 0, 512), (1, 0, 512)]
+STAGES = [(0, 0, 256), (0, 256, 256), (1, 0, 256), (1, 256, 256)]
 QCOLS = 128
 LOADS = [(0, 0, 256), (0, 256, 256), (1, 0, 256), (1, 256, 256)]
-STORES = [[(c, 1, 0, 512) for c in range(4)], [(0, 1, 0, 512), (1, 1, 0, 512), (2, 1, 0, 512), (3, 1, 0, 256), (3, 1, 256, 512)]]
+STORES = [[(0, 2, 0, 256), (2, 2, 0, 256)]] * 4
 
 
 def tile_rows_glin_gelu_bias_kernel(tc, x, w_words, w_scales, b, out):
@@ -46,13 +46,12 @@ def tile_rows_glin_gelu_bias_kernel(tc, x, w_words, w_scales, b, out):
         res = [keep.tile([P, TILES, w], F32, name="res%d" % i) for i, (s, c0, w) in enumerate(STAGES)]
         banks = [[psum.tile([M, N], F32, name="bank%d_%d" % (c, k)) for k in range(2)] for c in range(TILES)]
 
+        nc.vector.memset(b_rows[:], 0.0)
         nc.vector.memset(w_plane[:].rearrange("p s m -> p (s m)").bitcast(I32), 0)
         nc.vector.memset(warm_in[:], 0.0)
-        nc.gpsimd.memset(b_rows[:], 0.0)
-        nc.gpsimd.dma_start(
-            out=b_rows[0:P:32, :].rearrange("q (g i) -> q g i", i=32),
-            in_=b.rearrange("g (q i) o -> q g (i o)", i=32),
-        )
+        nc.vector.memset(x_codes[:, 0:pad], 0)
+        nc.vector.memset(x_plane[:, 0:pad].bitcast(I32), 0)
+        nc.sync.dma_start(out=w_codes[:].bitcast(I32), in_=w_words.rearrange("(s c) p b -> (c p) s b", c=TILES).bitcast(I32))
         nc.scalar.activation(out=warm_out[:], in_=warm_in[:], func=GELU)
 
         def load(i):
@@ -62,20 +61,24 @@ def tile_rows_glin_gelu_bias_kernel(tc, x, w_words, w_scales, b, out):
                 in_=x[s * TILES : (s + 1) * TILES].rearrange("c (p j) n -> (c p) j n", j=PACK)[:, :, c0 : c0 + w],
             )
 
-        for i in range(2):
+        for i in range(1):
             load(i)
-        nc.sync.dma_start(out=w_codes[:].bitcast(I32), in_=w_words.rearrange("(s c) p b -> (c p) s b", c=TILES).bitcast(I32))
+        nc.sync.dma_start(
+            out=b_rows[0:P:32, :].rearrange("q (g i) -> q g i", i=32),
+            in_=b.rearrange("g (q i) o -> q g (i o)", i=32),
+        )
         scale_rows = w_scales.rearrange("(s c) f m -> c f s m", c=TILES)
         for c in range(TILES):
             nc.sync.dma_start(out=w_plane[ROWS * c : ROWS * c + 4].bitcast(I32), in_=scale_rows[c].bitcast(I32))
-        for i in range(2, len(LOADS)):
+        for i in range(1, len(LOADS)):
             load(i)
 
         def quantise(k):
             s, c0, w = LOADS[k]
             parts = range(0, w, QCOLS)
             for q in parts:
-                nc.vector.tensor_copy(
+                copy = nc.scalar.copy if (k, q) in [(0, 128)] else nc.vector.tensor_copy
+                copy(
                     out=packed[k][:, q : q + QCOLS, :].rearrange("p (c i) t -> p c t i", i=4),
                     in_=raw[k][:, :, q : q + QCOLS].rearrange("p t (c i) -> p c t i", i=4),
                 )

@@ -19,31 +19,32 @@ PACK = 4
 ROWS = D // PACK
 TILES = P // ROWS
 SETS = G // TILES
-STAGES = [(0, 0, 256), (0, 256, 256), (1, 0, 256), (1, 256, 256)]
+WIDTHS = [[256,256],[256,256]]
 QCOLS = 128
-LOADS = [(0, 0, 256), (0, 256, 256), (1, 0, 256), (1, 256, 256)]
-STORES = [[(0, 2, 0, 256), (2, 2, 0, 256)]] * 4
+HELP = [96,64,0,0]
+STORES = [[1,1,1,1],[1,1,1,1],[1,1,1,1],[1,1,1,1]]
 
 
 def tile_rows_glin_gelu_bias_kernel(tc, x, w_words, w_scales, b, out):
     nc = tc.nc
-    pad = N - STAGES[0][2]
+    stages = [(s, sum(WIDTHS[s][:k]), w) for s in range(SETS) for k, w in enumerate(WIDTHS[s])]
+    pad = N - stages[0][2]
     with ExitStack() as ctx:
         keep = ctx.enter_context(tc.tile_pool(name="keep", bufs=1))
         psum = ctx.enter_context(tc.psum_pool(name="psum", bufs=1))
         ctx.enter_context(tc.manual_schedule())
 
-        w_codes = keep.tile([P, SETS, 2 * M], U8, align_bytes=64)
+        w_codes = [keep.tile([P, 2 * M], U8, align_bytes=64, name="w_codes%d" % s) for s in range(SETS)]
         w_plane = keep.tile([P, SETS, M], U8, align_bytes=64)
-        b_rows = keep.tile([P, G * 32], F32, align_bytes=64)
-        b_cols = keep.tile([P, G * 32], F32, align_bytes=64)
+        b_rows = keep.tile([P, 32], F32, align_bytes=64)
+        b_cols = keep.tile([P, 32], F32, align_bytes=64)
         x_codes = keep.tile([P, pad + SETS * N], U32, align_bytes=64)
         x_plane = keep.tile([P, pad + SETS * N], U8, align_bytes=64)
         warm_in = keep.tile([P, 1], F32)
         warm_out = keep.tile([P, 1], F32)
-        raw = [keep.tile([P, PACK, w], F32, name="raw%d" % i) for i, (s, c0, w) in enumerate(LOADS)]
-        packed = [keep.tile([P, w, PACK], BF16, align_bytes=64, name="packed%d" % i) for i, (s, c0, w) in enumerate(LOADS)]
-        res = [keep.tile([P, TILES, w], F32, name="res%d" % i) for i, (s, c0, w) in enumerate(STAGES)]
+        raw = [keep.tile([P, PACK, w], F32, name="raw%d" % i) for i, (s, c0, w) in enumerate(stages)]
+        packed = [keep.tile([P, w, PACK], BF16, align_bytes=64, name="packed%d" % i) for i, (s, c0, w) in enumerate(stages)]
+        res = [keep.tile([P, TILES, w], F32, name="res%d" % i) for i, (s, c0, w) in enumerate(stages)]
         banks = [[psum.tile([M, N], F32, name="bank%d_%d" % (c, k)) for k in range(2)] for c in range(TILES)]
 
         nc.vector.memset(b_rows[:], 0.0)
@@ -51,50 +52,60 @@ def tile_rows_glin_gelu_bias_kernel(tc, x, w_words, w_scales, b, out):
         nc.vector.memset(warm_in[:], 0.0)
         nc.vector.memset(x_codes[:, 0:pad], 0)
         nc.vector.memset(x_plane[:, 0:pad].bitcast(I32), 0)
-        nc.sync.dma_start(out=w_codes[:].bitcast(I32), in_=w_words.rearrange("(s c) p b -> (c p) s b", c=TILES).bitcast(I32))
-        nc.scalar.activation(out=warm_out[:], in_=warm_in[:], func=GELU)
 
         def load(i):
-            s, c0, w = LOADS[i]
+            s, c0, w = stages[i]
             nc.sync.dma_start(
                 out=raw[i][:],
                 in_=x[s * TILES : (s + 1) * TILES].rearrange("c (p j) n -> (c p) j n", j=PACK)[:, :, c0 : c0 + w],
             )
 
-        for i in range(1):
-            load(i)
-        nc.sync.dma_start(
-            out=b_rows[0:P:32, :].rearrange("q (g i) -> q g i", i=32),
-            in_=b.rearrange("g (q i) o -> q g (i o)", i=32),
-        )
-        scale_rows = w_scales.rearrange("(s c) f m -> c f s m", c=TILES)
+        def load_weights(queue, s):
+            queue.dma_start(out=w_codes[s][:].bitcast(I32), in_=w_words.rearrange("(s c) p b -> s (c p) b", c=TILES)[s].bitcast(I32))
+
+        def load_bias(queue):
+            queue.dma_start(out=b_rows[0:P:4, :], in_=b.rearrange("g (q i) o -> q g (i o)", i=32))
+
+        def load_scales(queue, c):
+            scale_rows = w_scales.rearrange("(s c) f m -> c f s m", c=TILES)
+            queue.dma_start(out=w_plane[ROWS * c : ROWS * c + 4].bitcast(I32), in_=scale_rows[c].bitcast(I32))
+
+        load_weights(nc.sync, 0)
+        nc.scalar.activation(out=warm_out[:], in_=warm_in[:], func=GELU)
+        load(0)
+        load_bias(nc.sync)
         for c in range(TILES):
-            nc.sync.dma_start(out=w_plane[ROWS * c : ROWS * c + 4].bitcast(I32), in_=scale_rows[c].bitcast(I32))
-        for i in range(1, len(LOADS)):
+            load_scales(nc.sync, c)
+        for i in range(1, len(stages)):
             load(i)
+        load_weights(nc.sync, 1)
+
+        def interleave(copy, k, lo, hi):
+            copy(
+                out=packed[k][:, lo:hi, :].rearrange("p (c i) t -> p c t i", i=4),
+                in_=raw[k][:, :, lo:hi].rearrange("p t (c i) -> p c t i", i=4),
+            )
 
         def quantise(k):
-            s, c0, w = LOADS[k]
-            parts = range(0, w, QCOLS)
-            for q in parts:
-                copy = nc.scalar.copy if (k, q) in [(0, 128)] else nc.vector.tensor_copy
-                copy(
-                    out=packed[k][:, q : q + QCOLS, :].rearrange("p (c i) t -> p c t i", i=4),
-                    in_=raw[k][:, :, q : q + QCOLS].rearrange("p t (c i) -> p c t i", i=4),
-                )
+            s, c0, w = stages[k]
+            parts = [(q, min(QCOLS, w - q)) for q in range(0, w, QCOLS)]
+            for q, n in parts:
+                if q < w - HELP[k]:
+                    interleave(nc.vector.tensor_copy, k, q, min(q + n, w - HELP[k]))
             start = pad + s * N + c0
-            for q in parts:
+            for q, n in parts:
                 nc.vector.quantize_mx(
-                    out=x_codes[:, start + q : start + q + QCOLS].bitcast(FP8X4),
-                    scales=x_plane[:, start + q : start + q + QCOLS],
-                    in_=packed[k][:, q : q + QCOLS, :].rearrange("p n t -> p (n t)"),
+                    out=x_codes[:, start + q : start + q + n].bitcast(FP8X4),
+                    scales=x_plane[:, start + q : start + q + n],
+                    in_=packed[k][:, q : q + n, :].rearrange("p n t -> p (n t)"),
                 )
 
-        done = 0
-        for i, (s, c0, w) in enumerate(STAGES):
-            while done < len(LOADS) and LOADS[done][0] * N + LOADS[done][1] < s * N + c0 + w:
-                quantise(done)
-                done += 1
+        for k, (s, c0, w) in enumerate(stages):
+            if HELP[k]:
+                interleave(nc.scalar.copy, k, w - HELP[k], w)
+
+        for i, (s, c0, w) in enumerate(stages):
+            quantise(i)
             if i == 0:
                 nc.vector.transpose(out=b_cols[:], in_=b_rows[:])
             end = pad + s * N + c0 + w
@@ -103,24 +114,26 @@ def tile_rows_glin_gelu_bias_kernel(tc, x, w_words, w_scales, b, out):
                 rows = slice(ROWS * c, ROWS * (c + 1))
                 nc.tensor.matmul_mx(
                     out=banks[c][i % 2][:],
-                    lhsT=w_codes[rows, s, :].bitcast(FP4X4),
+                    lhsT=w_codes[s][rows, :].bitcast(FP4X4),
                     lhsT_scale=w_plane[rows, s, :],
                     rhs=x_codes[rows, window].bitcast(FP8X4),
                     rhs_scale=x_plane[rows, window],
                     start=True,
                     stop=True,
                 )
-            for first, count, lo, hi in STORES[i]:
+            first = 0
+            for count in STORES[i]:
                 for c in range(first, first + count):
                     g = s * TILES + c
                     nc.scalar.activation(
-                        out=res[i][:, c, lo:hi],
-                        in_=banks[c][i % 2][:, N - w + lo : N - w + hi],
+                        out=res[i][:, c, :],
+                        in_=banks[c][i % 2][:, N - w : N],
                         func=GELU,
-                        bias=b_cols[:, 32 * g : 32 * g + 1],
+                        bias=b_cols[:, 4 * g : 4 * g + 1],
                     )
                 g0 = s * TILES + first
                 nc.sync.dma_start(
-                    out=out[g0 : g0 + count, :, c0 + lo : c0 + hi].rearrange("g m n -> m g n"),
-                    in_=res[i][:, first : first + count, lo:hi],
+                    out=out[g0 : g0 + count, :, c0 : c0 + w].rearrange("g m n -> m g n"),
+                    in_=res[i][:, first : first + count, :],
                 )
+                first = first + count

@@ -22,7 +22,7 @@ SETS = G // TILES
 WIDTHS = [[256,256],[256,256]]
 QCOLS = 128
 HELP = [96,64,0,0]
-STORES = [[1,1,1,1],[1,1,1,1],[1,1,1,1],[1,1,1,1]]
+STORES = [[1,1,1,1],[1,1,1,1],[2,2],[2,2]]
 
 
 def tile_rows_glin_gelu_bias_kernel(tc, x, w_words, w_scales, b, out):

@@ -21,7 +21,7 @@ TILES = P // ROWS
 SETS = G // TILES
 WIDTHS = [[256,256],[256,256]]
 QCOLS = 128
-HELP = [96,64,0,0]
+HELP = [0,0,0,0]
 STORES = [[1,1,1,1],[1,1,1,1],[2,2],[2,2]]
 
 
@@ -40,8 +40,6 @@ def tile_rows_glin_gelu_bias_kernel(tc, x, w_words, w_scales, b, out):
         b_cols = keep.tile([P, 32], F32, align_bytes=64)
         x_codes = keep.tile([P, pad + SETS * N], U32, align_bytes=64)
         x_plane = keep.tile([P, pad + SETS * N], U8, align_bytes=64)
-        warm_in = keep.tile([P, 1], F32)
-        warm_out = keep.tile([P, 1], F32)
         raw = [keep.tile([P, PACK, w], F32, name="raw%d" % i) for i, (s, c0, w) in enumerate(stages)]
         packed = [keep.tile([P, w, PACK], BF16, align_bytes=64, name="packed%d" % i) for i, (s, c0, w) in enumerate(stages)]
         res = [keep.tile([P, TILES, w], F32, name="res%d" % i) for i, (s, c0, w) in enumerate(stages)]
@@ -49,7 +47,6 @@ def tile_rows_glin_gelu_bias_kernel(tc, x, w_words, w_scales, b, out):
 
         nc.vector.memset(b_rows[:], 0.0)
         nc.vector.memset(w_plane[:].rearrange("p s m -> p (s m)").bitcast(I32), 0)
-        nc.vector.memset(warm_in[:], 0.0)
         nc.vector.memset(x_codes[:, 0:pad], 0)
         nc.vector.memset(x_plane[:, 0:pad].bitcast(I32), 0)
 
@@ -71,7 +68,6 @@ def tile_rows_glin_gelu_bias_kernel(tc, x, w_words, w_scales, b, out):
             queue.dma_start(out=w_plane[ROWS * c : ROWS * c + 4].bitcast(I32), in_=scale_rows[c].bitcast(I32))
 
         load_weights(nc.sync, 0)
-        nc.scalar.activation(out=warm_out[:], in_=warm_in[:], func=GELU)
         load(0)
         load_bias(nc.sync)
         for c in range(TILES):
@@ -92,6 +88,8 @@ def tile_rows_glin_gelu_bias_kernel(tc, x, w_words, w_scales, b, out):
             for q, n in parts:
                 if q < w - HELP[k]:
                     interleave(nc.vector.tensor_copy, k, q, min(q + n, w - HELP[k]))
+            if k == 0:
+                nc.vector.transpose(out=b_cols[:], in_=b_rows[:])
             start = pad + s * N + c0
             for q, n in parts:
                 nc.vector.quantize_mx(
@@ -106,8 +104,6 @@ def tile_rows_glin_gelu_bias_kernel(tc, x, w_words, w_scales, b, out):
 
         for i, (s, c0, w) in enumerate(stages):
             quantise(i)
-            if i == 0:
-                nc.vector.transpose(out=b_cols[:], in_=b_rows[:])
             end = pad + s * N + c0 + w
             window = slice(end - N, end)
             for c in range(TILES):

@@ -22,7 +22,7 @@ SETS = G // TILES
 WIDTHS = [[256,256],[256,256]]
 QCOLS = 128
 HELP = [0,0,0,0]
-STORES = [[1,1,1,1],[1,1,1,1],[2,2],[2,2]]
+STORES = [[1,1,1,1],[1,1,1,1],[2,2],[2,1,1]]
 
 
 def tile_rows_glin_gelu_bias_kernel(tc, x, w_words, w_scales, b, out):

@@ -34,15 +34,15 @@ def tile_rows_glin_gelu_bias_kernel(tc, x, w_words, w_scales, b, out):
         psum = ctx.enter_context(tc.psum_pool(name="psum", bufs=1))
         ctx.enter_context(tc.manual_schedule())
 
-        w_codes = [keep.tile([P, 2 * M], U8, align_bytes=64, name="w_codes%d" % s) for s in range(SETS)]
-        w_plane = keep.tile([P, SETS, M], U8, align_bytes=64)
+        w_codes = [keep.tile([P, 2 * M], U8, align_bytes=256, name="w_codes%d" % s) for s in range(SETS)]
+        w_plane = keep.tile([P, SETS, M], U8, align_bytes=256)
         b_rows = keep.tile([P, 32], F32, align_bytes=64)
         b_cols = keep.tile([P, 32], F32, align_bytes=64)
         x_codes = keep.tile([P, pad + SETS * N], U32, align_bytes=64)
         x_plane = keep.tile([P, pad + SETS * N], U8, align_bytes=64)
-        raw = [keep.tile([P, PACK, w], F32, name="raw%d" % i) for i, (s, c0, w) in enumerate(stages)]
+        raw = [keep.tile([P, PACK, w], F32, align_bytes=256, name="raw%d" % i) for i, (s, c0, w) in enumerate(stages)]
         packed = [keep.tile([P, w, PACK], BF16, align_bytes=64, name="packed%d" % i) for i, (s, c0, w) in enumerate(stages)]
-        res = [keep.tile([P, TILES, w], F32, name="res%d" % i) for i, (s, c0, w) in enumerate(stages)]
+        res = [keep.tile([P, TILES, w], F32, align_bytes=256, name="res%d" % i) for i, (s, c0, w) in enumerate(stages)]
         banks = [[psum.tile([M, N], F32, name="bank%d_%d" % (c, k)) for k in range(2)] for c in range(TILES)]
 
         nc.vector.memset(b_rows[:], 0.0)

@@ -19,10 +19,8 @@ PACK = 4
 ROWS = D // PACK
 TILES = P // ROWS
 SETS = G // TILES
-WIDTHS = [[256,256],[256,256]]
-QCOLS = 128
-HELP = [0,0,0,0]
-STORES = [[1,1,1,1],[1,1,1,1],[2,2],[2,1,1]]
+WIDTHS = [[128,192,192],[192,192,128]]
+STORES = [[2,2],[2,2],[2,2],[2,2],[2,2],[2,2]]
 
 
 def tile_rows_glin_gelu_bias_kernel(tc, x, w_words, w_scales, b, out):
@@ -34,9 +32,9 @@ def tile_rows_glin_gelu_bias_kernel(tc, x, w_words, w_scales, b, out):
         psum = ctx.enter_context(tc.psum_pool(name="psum", bufs=1))
         ctx.enter_context(tc.manual_schedule())
 
-        w_codes = [keep.tile([P, 2 * M], U8, align_bytes=256, name="w_codes%d" % s) for s in range(SETS)]
+        w_codes = keep.tile([P, SETS, 2 * M], U8, align_bytes=256)
         w_plane = keep.tile([P, SETS, M], U8, align_bytes=256)
-        b_rows = keep.tile([P, 32], F32, align_bytes=64)
+        b_rows = keep.tile([P, 32], F32, align_bytes=256)
         b_cols = keep.tile([P, 32], F32, align_bytes=64)
         x_codes = keep.tile([P, pad + SETS * N], U32, align_bytes=64)
         x_plane = keep.tile([P, pad + SETS * N], U8, align_bytes=64)
@@ -57,8 +55,8 @@ def tile_rows_glin_gelu_bias_kernel(tc, x, w_words, w_scales, b, out):
                 in_=x[s * TILES : (s + 1) * TILES].rearrange("c (p j) n -> (c p) j n", j=PACK)[:, :, c0 : c0 + w],
             )
 
-        def load_weights(queue, s):
-            queue.dma_start(out=w_codes[s][:].bitcast(I32), in_=w_words.rearrange("(s c) p b -> s (c p) b", c=TILES)[s].bitcast(I32))
+        def load_weights(queue):
+            queue.dma_start(out=w_codes[:].bitcast(I32), in_=w_words.rearrange("(s c) p b -> (c p) s b", c=TILES).bitcast(I32))
 
         def load_bias(queue):
             queue.dma_start(out=b_rows[0:P:4, :], in_=b.rearrange("g (q i) o -> q g (i o)", i=32))
@@ -67,14 +65,14 @@ def tile_rows_glin_gelu_bias_kernel(tc, x, w_words, w_scales, b, out):
             scale_rows = w_scales.rearrange("(s c) f m -> c f s m", c=TILES)
             queue.dma_start(out=w_plane[ROWS * c : ROWS * c + 4].bitcast(I32), in_=scale_rows[c].bitcast(I32))
 
-        load_weights(nc.sync, 0)
+        load_weights(nc.sync)
         load(0)
         load_bias(nc.sync)
+        load(1)
         for c in range(TILES):
             load_scales(nc.sync, c)
-        for i in range(1, len(stages)):
+        for i in range(2, len(stages)):
             load(i)
-        load_weights(nc.sync, 1)
 
         def interleave(copy, k, lo, hi):
             copy(
@@ -84,10 +82,9 @@ def tile_rows_glin_gelu_bias_kernel(tc, x, w_words, w_scales, b, out):
 
         def quantise(k):
             s, c0, w = stages[k]
-            parts = [(q, min(QCOLS, w - q)) for q in range(0, w, QCOLS)]
+            parts = [(0, w - 64), (w - 64, 64)]
             for q, n in parts:
-                if q < w - HELP[k]:
-                    interleave(nc.vector.tensor_copy, k, q, min(q + n, w - HELP[k]))
+                interleave(nc.vector.tensor_copy, k, q, q + n)
             if k == 0:
                 nc.vector.transpose(out=b_cols[:], in_=b_rows[:])
             start = pad + s * N + c0
@@ -98,10 +95,6 @@ def tile_rows_glin_gelu_bias_kernel(tc, x, w_words, w_scales, b, out):
                     in_=packed[k][:, q : q + n, :].rearrange("p n t -> p (n t)"),
                 )
 
-        for k, (s, c0, w) in enumerate(stages):
-            if HELP[k]:
-                interleave(nc.scalar.copy, k, w - HELP[k], w)
-
         for i, (s, c0, w) in enumerate(stages):
             quantise(i)
             end = pad + s * N + c0 + w
@@ -110,7 +103,7 @@ def tile_rows_glin_gelu_bias_kernel(tc, x, w_words, w_scales, b, out):
                 rows = slice(ROWS * c, ROWS * (c + 1))
                 nc.tensor.matmul_mx(
                     out=banks[c][i % 2][:],
-                    lhsT=w_codes[s][rows, :].bitcast(FP4X4),
+                    lhsT=w_codes[rows, s, :].bitcast(FP4X4),
                     lhsT_scale=w_plane[rows, s, :],
                     rhs=x_codes[rows, window].bitcast(FP8X4),
                     rhs_scale=x_plane[rows, window],

@@ -19,8 +19,8 @@ PACK = 4
 ROWS = D // PACK
 TILES = P // ROWS
 SETS = G // TILES
-WIDTHS = [[128,192,192],[192,192,128]]
-STORES = [[2,2],[2,2],[2,2],[2,2],[2,2],[2,2]]
+WIDTHS = [[128,128,128,128],[128,128,128,128]]
+STORES = [[4],[4],[4],[4],[4],[4],[4],[2,2]]
 
 
 def tile_rows_glin_gelu_bias_kernel(tc, x, w_words, w_scales, b, out):

@@ -19,14 +19,27 @@ PACK = 4
 ROWS = D // PACK
 TILES = P // ROWS
 SETS = G // TILES
-WIDTHS = [[128,128,128,128],[128,128,128,128]]
-STORES = [[4],[4],[4],[4],[4],[4],[4],[2,2]]
+PART = 64
+PARTS = SETS * N // PART
+LOADS = [[128,128,128,128],[128,128,128,128]]
+STEPS = [[128,128,128,128],[128,128,128,128]]
+STORES = [[128,128,128,128],[128,128,128,128]]
+
+
+def spans(widths):
+    return [(s, sum(widths[s][:k]), w) for s in range(SETS) for k, w in enumerate(widths[s])]
+
+
+def find(pieces, s, col):
+    return [i for i, (ps, c0, w) in enumerate(pieces) if ps == s and c0 <= col < c0 + w][0]
 
 
 def tile_rows_glin_gelu_bias_kernel(tc, x, w_words, w_scales, b, out):
     nc = tc.nc
-    stages = [(s, sum(WIDTHS[s][:k]), w) for s in range(SETS) for k, w in enumerate(WIDTHS[s])]
-    pad = N - stages[0][2]
+    loads = spans(LOADS)
+    steps = spans(STEPS)
+    stores = spans(STORES)
+    pad = N - steps[0][2]
     with ExitStack() as ctx:
         keep = ctx.enter_context(tc.tile_pool(name="keep", bufs=1))
         psum = ctx.enter_context(tc.psum_pool(name="psum", bufs=1))
@@ -38,9 +51,9 @@ def tile_rows_glin_gelu_bias_kernel(tc, x, w_words, w_scales, b, out):
         b_cols = keep.tile([P, 32], F32, align_bytes=64)
         x_codes = keep.tile([P, pad + SETS * N], U32, align_bytes=64)
         x_plane = keep.tile([P, pad + SETS * N], U8, align_bytes=64)
-        raw = [keep.tile([P, PACK, w], F32, align_bytes=256, name="raw%d" % i) for i, (s, c0, w) in enumerate(stages)]
-        packed = [keep.tile([P, w, PACK], BF16, align_bytes=64, name="packed%d" % i) for i, (s, c0, w) in enumerate(stages)]
-        res = [keep.tile([P, TILES, w], F32, align_bytes=256, name="res%d" % i) for i, (s, c0, w) in enumerate(stages)]
+        raw = [keep.tile([P, PACK, w], F32, align_bytes=256, name="raw%d" % i) for i, (s, c0, w) in enumerate(loads)]
+        packed = [keep.tile([P, PART, PACK], BF16, align_bytes=64, name="packed%d" % i) for i in range(PARTS)]
+        res = [keep.tile([P, TILES, w], F32, align_bytes=256, name="res%d" % i) for i, (s, c0, w) in enumerate(stores)]
         banks = [[psum.tile([M, N], F32, name="bank%d_%d" % (c, k)) for k in range(2)] for c in range(TILES)]
 
         nc.vector.memset(b_rows[:], 0.0)
@@ -49,7 +62,7 @@ def tile_rows_glin_gelu_bias_kernel(tc, x, w_words, w_scales, b, out):
         nc.vector.memset(x_plane[:, 0:pad].bitcast(I32), 0)
 
         def load(i):
-            s, c0, w = stages[i]
+            s, c0, w = loads[i]
             nc.sync.dma_start(
                 out=raw[i][:],
                 in_=x[s * TILES : (s + 1) * TILES].rearrange("c (p j) n -> (c p) j n", j=PACK)[:, :, c0 : c0 + w],
@@ -65,39 +78,29 @@ def tile_rows_glin_gelu_bias_kernel(tc, x, w_words, w_scales, b, out):
             scale_rows = w_scales.rearrange("(s c) f m -> c f s m", c=TILES)
             queue.dma_start(out=w_plane[ROWS * c : ROWS * c + 4].bitcast(I32), in_=scale_rows[c].bitcast(I32))
 
-        load_weights(nc.sync)
         load(0)
+        load_weights(nc.sync)
         load_bias(nc.sync)
         load(1)
-        for c in range(TILES):
+        for c in range(TILES - 1):
             load_scales(nc.sync, c)
-        for i in range(2, len(stages)):
+        load(2)
+        load_scales(nc.sync, TILES - 1)
+        for i in range(3, len(loads)):
             load(i)
 
-        def interleave(copy, k, lo, hi):
-            copy(
-                out=packed[k][:, lo:hi, :].rearrange("p (c i) t -> p c t i", i=4),
-                in_=raw[k][:, :, lo:hi].rearrange("p t (c i) -> p c t i", i=4),
+        def interleave(p):
+            s, col = divmod(p * PART, N)
+            src = find(loads, s, col)
+            off = col - loads[src][1]
+            nc.vector.tensor_copy(
+                out=packed[p][:].rearrange("p (c i) t -> p c t i", i=4),
+                in_=raw[src][:, :, off : off + PART].rearrange("p t (c i) -> p c t i", i=4),
             )
 
-        def quantise(k):
-            s, c0, w = stages[k]
-            parts = [(0, w - 64), (w - 64, 64)]
-            for q, n in parts:
-                interleave(nc.vector.tensor_copy, k, q, q + n)
-            if k == 0:
-                nc.vector.transpose(out=b_cols[:], in_=b_rows[:])
-            start = pad + s * N + c0
-            for q, n in parts:
-                nc.vector.quantize_mx(
-                    out=x_codes[:, start + q : start + q + n].bitcast(FP8X4),
-                    scales=x_plane[:, start + q : start + q + n],
-                    in_=packed[k][:, q : q + n, :].rearrange("p n t -> p (n t)"),
-                )
-
-        for i, (s, c0, w) in enumerate(stages):
-            quantise(i)
-            end = pad + s * N + c0 + w
+        def multiply(i):
+            s, col, width = steps[i]
+            end = pad + s * N + col + width
             window = slice(end - N, end)
             for c in range(TILES):
                 rows = slice(ROWS * c, ROWS * (c + 1))
@@ -110,19 +113,43 @@ def tile_rows_glin_gelu_bias_kernel(tc, x, w_words, w_scales, b, out):
                     start=True,
                     stop=True,
                 )
-            first = 0
-            for count in STORES[i]:
-                for c in range(first, first + count):
-                    g = s * TILES + c
-                    nc.scalar.activation(
-                        out=res[i][:, c, :],
-                        in_=banks[c][i % 2][:, N - w : N],
-                        func=GELU,
-                        bias=b_cols[:, 4 * g : 4 * g + 1],
-                    )
-                g0 = s * TILES + first
-                nc.sync.dma_start(
-                    out=out[g0 : g0 + count, :, c0 : c0 + w].rearrange("g m n -> m g n"),
-                    in_=res[i][:, first : first + count, :],
-                )
-                first = first + count
+
+        def activate(i):
+            s, col, width = steps[i]
+            for c in range(TILES):
+                g = s * TILES + c
+                for dst, (ds, c0, w) in enumerate(stores):
+                    lo, hi = max(col, c0), min(col + width, c0 + w)
+                    if ds == s and lo < hi:
+                        nc.scalar.activation(
+                            out=res[dst][:, c, lo - c0 : hi - c0],
+                            in_=banks[c][i % 2][:, N - (col + width - lo) : N - (col + width - hi)],
+                            func=GELU,
+                            bias=b_cols[:, 4 * g : 4 * g + 1],
+                        )
+                        count = 2 if dst == len(stores) - 1 else TILES
+                        if hi == c0 + w and (c + 1) % count == 0:
+                            nc.sync.dma_start(
+                                out=out[g + 1 - count : g + 1, :, c0 : c0 + w].rearrange("g m n -> m g n"),
+                                in_=res[dst][:, c + 1 - count : c + 1, :],
+                            )
+
+        def quantise(p):
+            start = pad + p * PART
+            nc.vector.quantize_mx(
+                out=x_codes[:, start : start + PART].bitcast(FP8X4),
+                scales=x_plane[:, start : start + PART],
+                in_=packed[p][:].rearrange("p n t -> p (n t)"),
+            )
+            for i, (s, col, width) in enumerate(steps):
+                if s * N + col + width == (p + 1) * PART:
+                    multiply(i)
+                    activate(i)
+
+        for p in range(0, PARTS, 2):
+            interleave(p)
+            interleave(p + 1)
+            if p == 0:
+                nc.vector.transpose(out=b_cols[:], in_=b_rows[:])
+            quantise(p)
+            quantise(p + 1)

from contextlib import ExitStack

import concourse.mybir as mybir

G, D, M, N = 8, 128, 128, 512
FLOPS = 2 * G * D * M * N

F32 = mybir.dt.float32
BF16 = mybir.dt.bfloat16
I32 = mybir.dt.int32
U32 = mybir.dt.uint32
U8 = mybir.dt.uint8
FP8X4 = mybir.dt.float8_e4m3fn_x4
FP4X4 = mybir.dt.float4_e2m1fn_x4
GELU = mybir.ActivationFunctionType.Gelu_apprx_tanh

P = 128
PACK = 4
ROWS = D // PACK
TILES = P // ROWS
SETS = G // TILES
PART = 64
PARTS = SETS * N // PART
LOADS = [[128,128,128,128],[128,128,128,128]]
STEPS = [[128,128,128,128],[128,128,128,128]]
STORES = [[128,128,128,128],[128,128,128,128]]


def spans(widths):
    return [(s, sum(widths[s][:k]), w) for s in range(SETS) for k, w in enumerate(widths[s])]


def find(pieces, s, col):
    return [i for i, (ps, c0, w) in enumerate(pieces) if ps == s and c0 <= col < c0 + w][0]


def tile_rows_glin_gelu_bias_kernel(tc, x, w_words, w_scales, b, out):
    nc = tc.nc
    loads = spans(LOADS)
    steps = spans(STEPS)
    stores = spans(STORES)
    pad = N - steps[0][2]
    with ExitStack() as ctx:
        keep = ctx.enter_context(tc.tile_pool(name="keep", bufs=1))
        psum = ctx.enter_context(tc.psum_pool(name="psum", bufs=1))
        ctx.enter_context(tc.manual_schedule())

        w_codes = keep.tile([P, SETS, 2 * M], U8, align_bytes=256)
        w_plane = keep.tile([P, SETS, M], U8, align_bytes=256)
        b_rows = keep.tile([P, 32], F32, align_bytes=256)
        b_cols = keep.tile([P, 32], F32, align_bytes=64)
        x_codes = keep.tile([P, pad + SETS * N], U32, align_bytes=64)
        x_plane = keep.tile([P, pad + SETS * N], U8, align_bytes=64)
        raw = [keep.tile([P, PACK, w], F32, align_bytes=256, name="raw%d" % i) for i, (s, c0, w) in enumerate(loads)]
        packed = [keep.tile([P, PART, PACK], BF16, align_bytes=64, name="packed%d" % i) for i in range(PARTS)]
        res = [keep.tile([P, TILES, w], F32, align_bytes=256, name="res%d" % i) for i, (s, c0, w) in enumerate(stores)]
        banks = [[psum.tile([M, N], F32, name="bank%d_%d" % (c, k)) for k in range(2)] for c in range(TILES)]

        nc.vector.memset(b_rows[:], 0.0)
        nc.vector.memset(w_plane[:].rearrange("p s m -> p (s m)").bitcast(I32), 0)
        nc.vector.memset(x_codes[:, 0:pad], 0)
        nc.vector.memset(x_plane[:, 0:pad].bitcast(I32), 0)

        def load(i):
            s, c0, w = loads[i]
            nc.sync.dma_start(
                out=raw[i][:],
                in_=x[s * TILES : (s + 1) * TILES].rearrange("c (p j) n -> (c p) j n", j=PACK)[:, :, c0 : c0 + w],
            )

        def load_weights(queue):
            queue.dma_start(out=w_codes[:].bitcast(I32), in_=w_words.rearrange("(s c) p b -> (c p) s b", c=TILES).bitcast(I32))

        def load_bias(queue):
            queue.dma_start(out=b_rows[0:P:4, :], in_=b.rearrange("g (q i) o -> q g (i o)", i=32))

        def load_scales(queue, c):
            scale_rows = w_scales.rearrange("(s c) f m -> c f s m", c=TILES)
            queue.dma_start(out=w_plane[ROWS * c : ROWS * c + 4].bitcast(I32), in_=scale_rows[c].bitcast(I32))

        load(0)
        load_weights(nc.sync)
        load_bias(nc.sync)
        load(1)
        for c in range(TILES - 1):
            load_scales(nc.sync, c)
        load(2)
        load_scales(nc.sync, TILES - 1)
        for i in range(3, len(loads)):
            load(i)

        def interleave(p):
            s, col = divmod(p * PART, N)
            src = find(loads, s, col)
            off = col - loads[src][1]
            nc.vector.tensor_copy(
                out=packed[p][:].rearrange("p (c i) t -> p c t i", i=4),
                in_=raw[src][:, :, off : off + PART].rearrange("p t (c i) -> p c t i", i=4),
            )

        def multiply(i):
            s, col, width = steps[i]
            end = pad + s * N + col + width
            window = slice(end - N, end)
            for c in range(TILES):
                rows = slice(ROWS * c, ROWS * (c + 1))
                nc.tensor.matmul_mx(
                    out=banks[c][i % 2][:],
                    lhsT=w_codes[rows, s, :].bitcast(FP4X4),
                    lhsT_scale=w_plane[rows, s, :],
                    rhs=x_codes[rows, window].bitcast(FP8X4),
                    rhs_scale=x_plane[rows, window],
                    start=True,
                    stop=True,
                )

        def activate(i):
            s, col, width = steps[i]
            for c in range(TILES):
                g = s * TILES + c
                for dst, (ds, c0, w) in enumerate(stores):
                    lo, hi = max(col, c0), min(col + width, c0 + w)
                    if ds == s and lo < hi:
                        nc.scalar.activation(
                            out=res[dst][:, c, lo - c0 : hi - c0],
                            in_=banks[c][i % 2][:, N - (col + width - lo) : N - (col + width - hi)],
                            func=GELU,
                            bias=b_cols[:, 4 * g : 4 * g + 1],
                        )
                        count = 2 if dst == len(stores) - 1 else TILES
                        if hi == c0 + w and (c + 1) % count == 0:
                            nc.sync.dma_start(
                                out=out[g + 1 - count : g + 1, :, c0 : c0 + w].rearrange("g m n -> m g n"),
                                in_=res[dst][:, c + 1 - count : c + 1, :],
                            )

        def quantise(p):
            start = pad + p * PART
            nc.vector.quantize_mx(
                out=x_codes[:, start : start + PART].bitcast(FP8X4),
                scales=x_plane[:, start : start + PART],
                in_=packed[p][:].rearrange("p n t -> p (n t)"),
            )
            for i, (s, col, width) in enumerate(steps):
                if s * N + col + width == (p + 1) * PART:
                    multiply(i)
                    activate(i)

        for p in range(0, PARTS, 2):
            interleave(p)
            interleave(p + 1)
            if p == 0:
                nc.vector.transpose(out=b_cols[:], in_=b_rows[:])
            quantise(p)
            quantise(p + 1)
